import numpy as np
import ml_dtypes


def mxq(x, axis, fmt="e4m3"):
    dtype, down = {"e4m3": (ml_dtypes.float8_e4m3fn, 7), "e5m2": (ml_dtypes.float8_e5m2, 14)}[fmt]
    v = np.moveaxis(np.asarray(x, np.float32).astype(ml_dtypes.bfloat16).astype(np.float64), axis, -1)
    blocks = v.reshape(v.shape[:-1] + (-1, 32))
    amax = np.abs(blocks).max(-1, keepdims=True)
    byte = np.maximum(np.where(amax > 0, np.frexp(amax)[1] - 1 + 127, 0) - down, 1)
    scale = np.exp2(byte - 127.0)
    codes = (blocks / scale).astype(np.float32).astype(dtype).astype(np.float64)
    return np.moveaxis((codes * scale).reshape(v.shape), -1, axis)


WIDE = False


def mx_kscale(k):
    if not WIDE:
        return np.ones(k)
    levels = np.array([10, -10, 5, -5, 0])
    if k % 512:
        return np.exp2(np.random.permutation(np.resize(levels, k // 32))).repeat(32)
    a = np.empty((k // 512, 16))
    for p in range(k // 512):
        a[p, :8] = np.random.permutation(np.resize(levels, 8))
        for g in range(8):
            far = levels[np.abs(levels - a[p, g]) >= 10]
            a[p, g + 8] = far[np.random.randint(len(far))]
    return np.exp2(a.ravel()).repeat(32)


def f64(x):
    return np.asarray(x).astype(np.float64)


def striped(idx):
    return np.tile(np.asarray(idx).reshape(-1, 16).T, (8, 1)).astype(np.uint16)


def unstriped(offs):
    return offs[:16].T.reshape(-1).astype(np.int64)


E2M1 = np.array([0.0, 0.5, 1.0, 1.5, 2.0, 3.0, 4.0, 6.0, -0.0, -0.5, -1.0, -1.5, -2.0, -3.0, -4.0, -6.0])


def pack_weight(w, fmt):
    k, n = w.shape
    w = f64(np.asarray(w, np.float32).astype(ml_dtypes.bfloat16)).reshape(k // 32, 32, n)
    amax = np.abs(w).max(1)
    if fmt == "e4m3":
        byte = np.frexp(amax)[1] - 1 + 127 - 7
    else:
        mant, ex = np.frexp(amax / 6.0)
        byte = np.where(mant > 0.5, ex, ex - 1) + 127
    byte = np.clip(np.where(amax > 0, byte, 1), 1, 254)
    scaled = (w * np.exp2(127.0 - byte)[:, None, :]).reshape(k, n).astype(np.float32)
    by_word = np.ascontiguousarray(scaled.reshape(k // 512, 128, 4, n).transpose(0, 1, 3, 2))
    if fmt == "e4m3":
        words = by_word.astype(ml_dtypes.float8_e4m3fn).view(np.uint8)
    else:
        c = by_word.astype(ml_dtypes.float4_e2m1fn).view(np.uint8) & 0xF
        words = (c[..., 0::2] | (c[..., 1::2] << 4)).reshape(k // 512, 128, 2 * n)
    return np.ascontiguousarray(words), np.ascontiguousarray(byte.astype(np.uint8).reshape(k // 512, 16, n))


def unpack_weight(words, scales, fmt):
    g, _, n = scales.shape
    words = np.ascontiguousarray(words).reshape(g, 128, n, -1)
    if fmt == "e4m3":
        vals = words.view(ml_dtypes.float8_e4m3fn).astype(np.float64)
    else:
        nib = np.empty((g, 128, n, 4), np.uint8)
        nib[..., 0::2] = words & 0xF
        nib[..., 1::2] = words >> 4
        vals = E2M1[nib]
    vals = vals * np.repeat(np.exp2(scales.astype(np.float64) - 127.0), 8, axis=1)[..., None]
    return vals.transpose(0, 1, 3, 2).reshape(g * 512, n)


def sigmoid(v):
    return 1.0 / (1.0 + np.exp(-v))


def bf(x):
    return np.asarray(x, np.float32).astype(ml_dtypes.bfloat16)


def planes(Y):
    r, m = Y.shape
    b = f64(bf(Y)).reshape(r // 32, 32, m)
    amax = np.abs(b).max(1)
    byte = np.clip(np.where(amax > 0, np.frexp(amax)[1] - 1 + 127 - 7, 1), 1, 254)
    codes = (b * np.exp2(127.0 - byte)[:, None, :]).reshape(r, m).astype(np.float32).astype(ml_dtypes.float8_e4m3fn).view(np.uint8)
    words = codes.reshape(r // 512, 128, 4, m).transpose(0, 1, 3, 2)
    return np.ascontiguousarray(words), np.ascontiguousarray(byte.astype(np.uint8).reshape(r // 512, 16, m))


K, R, F, T, J, G = 512, 512, 512, 2048, 512, 64


def setup_inputs():
    n = np.random.standard_normal
    idx = np.random.permutation(T)[:J]
    fk = mx_kscale(K)
    fr = mx_kscale(R)
    dtabp = pack_weight(n((K, T)) / fk[:, None], "e4m3")
    tabp = pack_weight(n((K, T)) / fk[:, None], "e4m3")
    return {
        "dtab_words": dtabp[0],
        "dtab_scales": dtabp[1],
        "tab_words": tabp[0],
        "tab_scales": tabp[1],
        "w1": (n((K, R)) * 1 / np.sqrt(K) * fk[:, None]).astype(np.float32),
        "steep": (np.random.uniform(1.0, 4.0, (R, 1))).astype(np.float32),
        "rs": (np.random.uniform(0.5, 2.0, (R, 1)) * fr[:, None]).astype(np.float32),
        "wor": (n((R, F)) * 1 / np.sqrt(R) / fr[:, None]).astype(np.float32),
        "res": (n((F, G)) * 0.5).astype(np.float32),
        "offs": striped(idx),
    }


def reference(dtab_words, dtab_scales, tab_words, tab_scales, w1, steep, rs, wor, res, offs):
    idx = unstriped(offs)
    dtabu = unpack_weight(dtab_words, dtab_scales, "e4m3")
    tabu = unpack_weight(tab_words, tab_scales, "e4m3")
    w1q = mxq(f64(w1), 0, "e4m3")
    tabidxg = tabu[:, idx]
    a = w1q.T @ tabidxg
    dtabidxg = dtabu[:, idx]
    ta = w1q.T @ dtabidxg
    h1 = np.tanh(a)
    p = sigmoid(a * f64(steep))
    z = p.reshape(R, G, J // G).sum(axis=2)
    th1 = ta * (1.0 - np.square(h1))
    tp = ta * f64(steep) * p * (1.0 - p)
    tz = tp.reshape(R, G, J // G).sum(axis=2)
    tu1 = ((tp * h1 + th1 * p).reshape(R, G, J // G).sum(axis=2) - tz * (p * h1).reshape(R, G, J // G).sum(axis=2) / z) / z
    fo1 = tu1 * f64(rs)
    worq = mxq(f64(wor), 0, "e4m3")
    fo1q = mxq(fo1, 0, "e4m3")
    yo = worq.T @ fo1q
    y = yo + f64(res)
    words, scales = planes(y)
    return y, words, scales

@@ -1,0 +1,205 @@
+from contextlib import ExitStack
+
+import concourse.mybir as mybir
+from concourse.masks import make_identity
+
+F32 = mybir.dt.float32
+BF16 = mybir.dt.bfloat16
+I32 = mybir.dt.int32
+U32 = mybir.dt.uint32
+U16 = mybir.dt.uint16
+U8 = mybir.dt.uint8
+FP8X4 = mybir.dt.float8_e4m3fn_x4
+ALU = mybir.AluOpType
+ACT = mybir.ActivationFunctionType
+
+P = 128
+PACK = 4
+K, R, F, T, J, G = 512, 512, 512, 2048, 512, 64
+VOTE = J // G
+HALVES = 2
+PAIR = PACK // HALVES
+DTAB_PLANE = 4
+W1_SCALAR_SHARE = 48
+
+FLOPS = 2 * K * R * J * 2 + 2 * R * F * G
+
+
+def dealt_views(raw, grouped, m0, m1):
+    src = raw[:].rearrange("p t (m j) -> p m t j", j=PACK)[:, m0:m1]
+    dst = grouped[:].rearrange("p (j m t) -> p m t j", j=PACK, t=PACK)[:, m0:m1]
+    return dst, src
+
+
+def tile_attend_tgroupvote_o_pl_kernel(tc, dtab_words, dtab_scales, tab_words, tab_scales, w1, steep, rs, wor, res, offs,
+                                        out_0, out_1, out_2):
+    nc = tc.nc
+    with ExitStack() as ctx:
+        keep = ctx.enter_context(tc.tile_pool(name="keep", bufs=1))
+        work = ctx.enter_context(tc.tile_pool(name="work", bufs=HALVES))
+        psum = ctx.enter_context(tc.psum_pool(name="psum", bufs=1))
+
+        offsets = keep.tile([P, J // 16], U16, name="offsets")
+        nc.sync.dma_start(offsets[:], offs)
+        w1_raw = keep.tile([P, PACK, R], F32, name="w1_raw", tag="weights_raw")
+        nc.sync.dma_start(w1_raw[:], w1.rearrange("(p t) r -> p t r", t=PACK))
+        tab_w = keep.tile([P, T], I32, name="tab_w")
+        nc.sync.dma_start(tab_w[:], tab_words[0].rearrange("p n t -> p (n t)").bitcast(I32))
+        dtab_w = keep.tile([P, T], I32, name="dtab_w")
+        nc.sync.dma_start(dtab_w[:], dtab_words[0].rearrange("p n t -> p (n t)").bitcast(I32))
+        steep_sb = keep.tile([P, PACK], F32, name="steep_sb")
+        nc.scalar.dma_start(steep_sb[:], steep.rearrange("(p t) o -> p (t o)", t=PACK))
+
+        tab_s = keep.tile([P, T], U8, name="tab_s", tag="tab_s_then_res")
+        dtab_s = keep.tile([P, T], U8, name="dtab_s", tag="dtab_s_then_rs")
+        nc.vector.memset(tab_s[:].bitcast(I32), 0)
+        nc.vector.memset(dtab_s[:].bitcast(I32), 0)
+        for quad in range(4):
+            nc.scalar.dma_start(tab_s[32 * quad:32 * quad + 4, :].bitcast(I32),
+                                tab_scales[0, 4 * quad:4 * quad + 4, :].bitcast(I32))
+        for quad in range(4):
+            first = 32 * quad + DTAB_PLANE
+            nc.gpsimd.dma_start(dtab_s[first:first + 4, :].bitcast(I32),
+                                dtab_scales[0, 4 * quad:4 * quad + 4, :].bitcast(I32))
+
+        identity = keep.tile([P, P], F32, name="identity")
+        make_identity(nc, identity[:])
+        neg_steep = keep.tile([P, PACK], F32, name="neg_steep")
+        nc.vector.tensor_scalar(neg_steep[:], steep_sb[:], -1.0, None, ALU.mult)
+
+        tab_gs = keep.tile([P, J], U8, name="tab_gs", align_bytes=64)
+        nc.vector.tensor_copy(tab_gs[:], tab_s[:].indirect(offsets[:]))
+
+        w1_grouped = keep.tile([P, PACK * R], BF16, name="w1_grouped", align_bytes=64)
+        dst, src = dealt_views(w1_raw, w1_grouped, 0, W1_SCALAR_SHARE)
+        nc.scalar.copy(dst, src)
+        dst, src = dealt_views(w1_raw, w1_grouped, W1_SCALAR_SHARE, P)
+        nc.vector.tensor_copy(dst, src)
+        w1_codes = keep.tile([P, R], U32, name="w1_codes", align_bytes=64)
+        w1_scales = keep.tile([P, R], U8, name="w1_scales", align_bytes=64)
+        nc.vector.quantize_mx(w1_codes[:].bitcast(FP8X4), w1_scales[:], w1_grouped[:])
+
+        tab_gw = keep.tile([P, J], U32, name="tab_gw", align_bytes=64)
+        nc.vector.tensor_copy(tab_gw[:], tab_w[:].bitcast(U32).indirect(offsets[:]))
+        dtab_gs = keep.tile([P, J], U8, name="dtab_gs", align_bytes=64)
+        nc.vector.tensor_copy(dtab_gs[:], dtab_s[:].indirect(offsets[:]))
+        dtab_gw = keep.tile([P, J], U32, name="dtab_gw", align_bytes=64)
+        nc.vector.tensor_copy(dtab_gw[:], dtab_w[:].bitcast(U32).indirect(offsets[:]))
+
+        wor_raw = keep.tile([P, PACK, F], F32, name="wor_raw", tag="weights_raw")
+        nc.sync.dma_start(wor_raw[:], wor.rearrange("(p t) f -> p t f", t=PACK))
+        res_sb = keep.tile([P, PACK, G], F32, name="res_sb", tag="tab_s_then_res")
+        nc.sync.dma_start(res_sb[:], res.rearrange("(p j) g -> p j g", j=PACK))
+        rs_sb = keep.tile([P, PACK], F32, name="rs_sb", tag="dtab_s_then_rs")
+        nc.sync.dma_start(rs_sb[:], rs.rearrange("(p t) o -> p (t o)", t=PACK))
+
+        z_bank = psum.tile([P, HALVES, P], F32, name="z_bank")
+        bn_bank = psum.tile([P, HALVES, 2, P], F32, name="bn_bank")
+        acc_bank = psum.tile([P, HALVES, P], F32, name="acc_bank")
+        back_bank = psum.tile([P, 2, PACK, G], F32, name="back_bank")
+        weight = keep.tile([P, PACK, G], F32, name="weight")
+
+        def group_sum(out, terms):
+            count = len(terms) * VOTE
+            n = 0
+            for term in terms:
+                for i in range(VOTE):
+                    nc.tensor.matmul(out, term[:, i].rearrange("p t g -> p (t g)"), identity[:], is_transpose=True,
+                                     start=(n == 0), stop=(n == count - 1))
+                    n = n + 1
+
+        def first_layer(name, t, words, plane):
+            bank = psum.tile([P, J], F32, name=name, bufs=2)
+            cols = slice(t * P, (t + 1) * P)
+            nc.tensor.matmul_mx(bank[:], w1_codes[:, cols].bitcast(FP8X4), w1_scales[:, cols],
+                                words[:].bitcast(FP8X4), plane, start=True, stop=True)
+            return bank[:].rearrange("p (g i) -> p i g", i=VOTE)
+
+        def flat(tile):
+            return tile[:].rearrange("p i t g -> p (i t g)")
+
+        for half in range(HALVES):
+            shape = [P, VOTE, PAIR, G]
+            p = work.tile(shape, F32, name="p")
+            h = work.tile(shape, F32, name="h")
+            slope = work.tile(shape, F32, name="slope")
+            h2 = work.tile(shape, F32, name="h2")
+            q = work.tile(shape, F32, name="q")
+            ph = work.tile(shape, F32, name="ph")
+            tpn = work.tile(shape, F32, name="tpn")
+            thp = work.tile(shape, F32, name="thp")
+            tph = work.tile(shape, F32, name="tph")
+            for t2 in range(PAIR):
+                t = PAIR * half + t2
+                a = first_layer("a_bank", t, tab_gw, tab_gs[:])
+                nc.scalar.activation(p[:, :, t2, :], a, ACT.Sigmoid, scale=steep_sb[:, t:t + 1])
+                nc.scalar.activation(h[:, :, t2, :], a, ACT.Tanh)
+            for t2 in range(PAIR):
+                t = PAIR * half + t2
+                nc.scalar.activation(slope[:, :, t2, :], p[:, :, t2, :], ACT.Identity,
+                                     scale=steep_sb[:, t:t + 1], bias=neg_steep[:, t:t + 1])
+            nc.scalar.activation(flat(h2), flat(h), ACT.Square)
+            group_sum(z_bank[:, half, :], [p])
+            for t2 in range(PAIR):
+                t = PAIR * half + t2
+                ta = first_layer("ta_bank", t, dtab_gw, dtab_gs[DTAB_PLANE:P, :])
+                nc.vector.tensor_tensor(q[:, :, t2, :], ta, p[:, :, t2, :], ALU.mult)
+            nc.vector.tensor_tensor(flat(ph), flat(p), flat(h), ALU.mult)
+            group_sum(bn_bank[:, half, 0, :], [ph])
+            nc.vector.tensor_tensor(flat(tpn), flat(slope), flat(q), ALU.mult)
+            group_sum(bn_bank[:, half, 1, :], [tpn])
+            rz = work.tile([P, P], F32, name="rz")
+            nc.vector.reciprocal(rz[:], z_bank[:, half, :])
+            nc.tensor.transpose(back_bank[:, 0, PAIR * half:PAIR * (half + 1), :].rearrange("p t g -> p (t g)"),
+                                rz[:], identity[:])
+            nc.vector.scalar_tensor_tensor(flat(thp), flat(h2), 1.0, flat(q), ALU.subtract, ALU.mult)
+            mean = work.tile([P, P], F32, name="mean")
+            nc.vector.tensor_tensor(mean[:], bn_bank[:, half, 0, :], rz[:], ALU.mult)
+            for part in range(2):
+                rows = slice(part * VOTE // 2, (part + 1) * VOTE // 2)
+                nc.vector.tensor_tensor(tph[:, rows], tpn[:, rows], h[:, rows], ALU.mult)
+            group_sum(acc_bank[:, half, :], [thp, tph])
+            shift = work.tile([P, P], F32, name="shift")
+            nc.vector.tensor_tensor(shift[:], bn_bank[:, half, 1, :], mean[:], ALU.mult)
+            numer = work.tile([P, P], F32, name="numer")
+            nc.vector.tensor_tensor(numer[:], shift[:], acc_bank[:, half, :], ALU.subtract)
+            for t2 in range(PAIR):
+                t = PAIR * half + t2
+                nc.scalar.activation(weight[:, t, :], back_bank[:, 0, t, :], ACT.Copy, scale=rs_sb[:, t:t + 1])
+            nc.tensor.transpose(back_bank[:, 1, PAIR * half:PAIR * (half + 1), :].rearrange("p t g -> p (t g)"),
+                                numer[:], identity[:])
+
+        wor_grouped = keep.tile([P, PACK * F], BF16, name="wor_grouped", align_bytes=64)
+        dst, src = dealt_views(wor_raw, wor_grouped, 0, P)
+        nc.scalar.copy(dst, src)
+        wor_codes = keep.tile([P, F], U32, name="wor_codes", align_bytes=64)
+        wor_scales = keep.tile([P, F], U8, name="wor_scales", align_bytes=64)
+        nc.vector.quantize_mx(wor_codes[:].bitcast(FP8X4), wor_scales[:], wor_grouped[:])
+
+        fo_grouped = keep.tile([P, G, PACK], BF16, name="fo_grouped", align_bytes=64)
+        nc.vector.tensor_tensor(fo_grouped[:], back_bank[:, 1].rearrange("p t g -> p g t"),
+                                weight[:].rearrange("p t g -> p g t"), ALU.mult)
+        fo_codes = keep.tile([P, G], U32, name="fo_codes", align_bytes=64)
+        fo_scales = keep.tile([P, G], U8, name="fo_scales", align_bytes=64)
+        nc.vector.quantize_mx(fo_codes[:].bitcast(FP8X4), fo_scales[:], fo_grouped[:].rearrange("p g t -> p (g t)"))
+
+        yo = psum.tile([P, PACK, G], F32, name="a_bank", bufs=2)
+        for j in range(PACK):
+            cols = slice(j * P, (j + 1) * P)
+            nc.tensor.matmul_mx(yo[:, j, :], wor_codes[:, cols].bitcast(FP8X4), wor_scales[:, cols],
+                                fo_codes[:].bitcast(FP8X4), fo_scales[:], start=True, stop=True)
+
+        y_grouped = keep.tile([P, G, PACK], BF16, name="y_grouped", align_bytes=64)
+        nc.vector.tensor_tensor(y_grouped[:], yo[:].rearrange("p j g -> p g j"),
+                                res_sb[:].rearrange("p j g -> p g j"), ALU.add)
+        y = keep.tile([P, PACK, G], F32, name="y")
+        nc.vector.tensor_tensor(y[:], yo[:], res_sb[:], ALU.add)
+        nc.sync.dma_start(out_0.rearrange("(p j) g -> p j g", j=PACK), y[:])
+        y_codes = keep.tile([P, G], I32, name="y_codes", align_bytes=64)
+        y_scales = keep.tile([P, G], U8, name="y_scales", align_bytes=64)
+        nc.vector.quantize_mx(y_codes[:].bitcast(FP8X4), y_scales[:], y_grouped[:].rearrange("p g j -> p (g j)"))
+        nc.scalar.dma_start(out_1[0].rearrange("p c t -> p (c t)").bitcast(I32), y_codes[:])
+        for quad in range(4):
+            queue = nc.sync if quad % 2 == 0 else nc.scalar
+            queue.dma_start(out_2[0, 4 * quad:4 * quad + 4, :].bitcast(I32),
+                            y_scales[32 * quad:32 * quad + 4, :].bitcast(I32))

@@ -19,8 +19,8 @@ K, R, F, T, J, G = 512, 512, 512, 2048, 512, 64
 VOTE = J // G
 HALVES = 2
 PAIR = PACK // HALVES
-DTAB_PLANE = 4
-W1_SCALAR_SHARE = 48
+SPREAD = 8
+W1_SCALAR_SHARE = 64
 
 FLOPS = 2 * K * R * J * 2 + 2 * R * F * G
 
@@ -39,40 +39,42 @@ def tile_attend_tgroupvote_o_pl_kernel(tc, dtab_words, dtab_scales, tab_words, t
         work = ctx.enter_context(tc.tile_pool(name="work", bufs=HALVES))
         psum = ctx.enter_context(tc.psum_pool(name="psum", bufs=1))
 
-        offsets = keep.tile([P, J // 16], U16, name="offsets")
-        nc.sync.dma_start(offsets[:], offs)
         w1_raw = keep.tile([P, PACK, R], F32, name="w1_raw", tag="weights_raw")
         nc.sync.dma_start(w1_raw[:], w1.rearrange("(p t) r -> p t r", t=PACK))
-        tab_w = keep.tile([P, T], I32, name="tab_w")
+        offsets = keep.tile([P, J // 16], U16, name="offsets")
+        nc.sync.dma_start(offsets[:], offs)
+        tab_w = keep.tile([P, T], I32, name="tab_w", tag="tab_w_then_res")
         nc.sync.dma_start(tab_w[:], tab_words[0].rearrange("p n t -> p (n t)").bitcast(I32))
-        dtab_w = keep.tile([P, T], I32, name="dtab_w")
+        dtab_w = keep.tile([P, T], I32, name="dtab_w", tag="dtab_w_then_rs")
         nc.sync.dma_start(dtab_w[:], dtab_words[0].rearrange("p n t -> p (n t)").bitcast(I32))
         steep_sb = keep.tile([P, PACK], F32, name="steep_sb")
         nc.scalar.dma_start(steep_sb[:], steep.rearrange("(p t) o -> p (t o)", t=PACK))
 
-        tab_s = keep.tile([P, T], U8, name="tab_s", tag="tab_s_then_res")
-        dtab_s = keep.tile([P, T], U8, name="dtab_s", tag="dtab_s_then_rs")
+        tab_s = keep.tile([P, T], U8, name="tab_s")
+        dtab_s = keep.tile([P, T], U8, name="dtab_s")
         nc.vector.memset(tab_s[:].bitcast(I32), 0)
+        planes = keep.tile([P, 2, J], U8, name="planes", align_bytes=64)
+        nc.vector.memset(planes[:].rearrange("p s j -> p (s j)").bitcast(I32), 0)
         nc.vector.memset(dtab_s[:].bitcast(I32), 0)
-        for quad in range(4):
-            nc.scalar.dma_start(tab_s[32 * quad:32 * quad + 4, :].bitcast(I32),
-                                tab_scales[0, 4 * quad:4 * quad + 4, :].bitcast(I32))
-        for quad in range(4):
-            first = 32 * quad + DTAB_PLANE
-            nc.gpsimd.dma_start(dtab_s[first:first + 4, :].bitcast(I32),
-                                dtab_scales[0, 4 * quad:4 * quad + 4, :].bitcast(I32))
+        nc.scalar.dma_start(tab_s[0:P:SPREAD, :].bitcast(I32), tab_scales[0].bitcast(I32))
+        nc.scalar.dma_start(dtab_s[0:P:SPREAD, :].bitcast(I32), dtab_scales[0].bitcast(I32))
 
         identity = keep.tile([P, P], F32, name="identity")
         make_identity(nc, identity[:])
         neg_steep = keep.tile([P, PACK], F32, name="neg_steep")
         nc.vector.tensor_scalar(neg_steep[:], steep_sb[:], -1.0, None, ALU.mult)
 
-        tab_gs = keep.tile([P, J], U8, name="tab_gs", align_bytes=64)
-        nc.vector.tensor_copy(tab_gs[:], tab_s[:].indirect(offsets[:]))
-
         w1_grouped = keep.tile([P, PACK * R], BF16, name="w1_grouped", align_bytes=64)
         dst, src = dealt_views(w1_raw, w1_grouped, 0, W1_SCALAR_SHARE)
         nc.scalar.copy(dst, src)
+
+        listed_s = keep.tile([P, 2, J], U8, name="listed_s")
+        nc.vector.tensor_copy(listed_s[:, 0, :], tab_s[:].indirect(offsets[:]))
+        nc.vector.tensor_copy(listed_s[:, 1, :], dtab_s[:].indirect(offsets[:]))
+        for row in range(4):
+            nc.scalar.dma_start(planes[row:P:32].rearrange("p s j -> p (s j)").bitcast(I32),
+                                listed_s[SPREAD * row:P:32].rearrange("p s j -> p (s j)").bitcast(I32))
+
         dst, src = dealt_views(w1_raw, w1_grouped, W1_SCALAR_SHARE, P)
         nc.vector.tensor_copy(dst, src)
         w1_codes = keep.tile([P, R], U32, name="w1_codes", align_bytes=64)
@@ -81,32 +83,30 @@ def tile_attend_tgroupvote_o_pl_kernel(tc, dtab_words, dtab_scales, tab_words, t
 
         tab_gw = keep.tile([P, J], U32, name="tab_gw", align_bytes=64)
         nc.vector.tensor_copy(tab_gw[:], tab_w[:].bitcast(U32).indirect(offsets[:]))
-        dtab_gs = keep.tile([P, J], U8, name="dtab_gs", align_bytes=64)
-        nc.vector.tensor_copy(dtab_gs[:], dtab_s[:].indirect(offsets[:]))
         dtab_gw = keep.tile([P, J], U32, name="dtab_gw", align_bytes=64)
         nc.vector.tensor_copy(dtab_gw[:], dtab_w[:].bitcast(U32).indirect(offsets[:]))
 
         wor_raw = keep.tile([P, PACK, F], F32, name="wor_raw", tag="weights_raw")
         nc.sync.dma_start(wor_raw[:], wor.rearrange("(p t) f -> p t f", t=PACK))
-        res_sb = keep.tile([P, PACK, G], F32, name="res_sb", tag="tab_s_then_res")
+        res_sb = keep.tile([P, PACK, G], F32, name="res_sb", tag="tab_w_then_res")
         nc.sync.dma_start(res_sb[:], res.rearrange("(p j) g -> p j g", j=PACK))
-        rs_sb = keep.tile([P, PACK], F32, name="rs_sb", tag="dtab_s_then_rs")
+        rs_sb = keep.tile([P, PACK], F32, name="rs_sb", tag="dtab_w_then_rs")
         nc.sync.dma_start(rs_sb[:], rs.rearrange("(p t) o -> p (t o)", t=PACK))
 
-        z_bank = psum.tile([P, HALVES, P], F32, name="z_bank")
-        bn_bank = psum.tile([P, HALVES, 2, P], F32, name="bn_bank")
-        acc_bank = psum.tile([P, HALVES, P], F32, name="acc_bank")
+        z_bank = psum.tile([P, HALVES + 1, P], F32, name="z_bank")
+        bn_bank = psum.tile([P, 2, HALVES, P], F32, name="bn_bank")
+        acc_bank = psum.tile([P, P], F32, name="acc_bank")
+        acc = [z_bank[:, HALVES, :], acc_bank[:]]
         back_bank = psum.tile([P, 2, PACK, G], F32, name="back_bank")
         weight = keep.tile([P, PACK, G], F32, name="weight")
 
-        def group_sum(out, terms):
-            count = len(terms) * VOTE
-            n = 0
-            for term in terms:
-                for i in range(VOTE):
-                    nc.tensor.matmul(out, term[:, i].rearrange("p t g -> p (t g)"), identity[:], is_transpose=True,
-                                     start=(n == 0), stop=(n == count - 1))
-                    n = n + 1
+        def group_sum(out, rows):
+            for n, row in enumerate(rows):
+                nc.tensor.matmul(out, row.rearrange("p t g -> p (t g)"), identity[:], is_transpose=True,
+                                 start=(n == 0), stop=(n == len(rows) - 1))
+
+        def slots(tile, first=0, last=VOTE):
+            return [tile[:, i] for i in range(first, last)]
 
         def first_layer(name, t, words, plane):
             bank = psum.tile([P, J], F32, name=name, bufs=2)
@@ -131,7 +131,7 @@ def tile_attend_tgroupvote_o_pl_kernel(tc, dtab_words, dtab_scales, tab_words, t
             tph = work.tile(shape, F32, name="tph")
             for t2 in range(PAIR):
                 t = PAIR * half + t2
-                a = first_layer("a_bank", t, tab_gw, tab_gs[:])
+                a = first_layer("a_bank", t, tab_gw, planes[:, 0, :])
                 nc.scalar.activation(p[:, :, t2, :], a, ACT.Sigmoid, scale=steep_sb[:, t:t + 1])
                 nc.scalar.activation(h[:, :, t2, :], a, ACT.Tanh)
             for t2 in range(PAIR):
@@ -139,39 +139,56 @@ def tile_attend_tgroupvote_o_pl_kernel(tc, dtab_words, dtab_scales, tab_words, t
                 nc.scalar.activation(slope[:, :, t2, :], p[:, :, t2, :], ACT.Identity,
                                      scale=steep_sb[:, t:t + 1], bias=neg_steep[:, t:t + 1])
             nc.scalar.activation(flat(h2), flat(h), ACT.Square)
-            group_sum(z_bank[:, half, :], [p])
+            group_sum(z_bank[:, half, :], slots(p))
             for t2 in range(PAIR):
                 t = PAIR * half + t2
-                ta = first_layer("ta_bank", t, dtab_gw, dtab_gs[DTAB_PLANE:P, :])
+                ta = first_layer("ta_bank", t, dtab_gw, planes[:, 1, :])
                 nc.vector.tensor_tensor(q[:, :, t2, :], ta, p[:, :, t2, :], ALU.mult)
             nc.vector.tensor_tensor(flat(ph), flat(p), flat(h), ALU.mult)
-            group_sum(bn_bank[:, half, 0, :], [ph])
+            group_sum(bn_bank[:, 0, half, :], slots(ph))
             nc.vector.tensor_tensor(flat(tpn), flat(slope), flat(q), ALU.mult)
-            group_sum(bn_bank[:, half, 1, :], [tpn])
-            rz = work.tile([P, P], F32, name="rz")
-            nc.vector.reciprocal(rz[:], z_bank[:, half, :])
-            nc.tensor.transpose(back_bank[:, 0, PAIR * half:PAIR * (half + 1), :].rearrange("p t g -> p (t g)"),
-                                rz[:], identity[:])
-            nc.vector.scalar_tensor_tensor(flat(thp), flat(h2), 1.0, flat(q), ALU.subtract, ALU.mult)
-            mean = work.tile([P, P], F32, name="mean")
-            nc.vector.tensor_tensor(mean[:], bn_bank[:, half, 0, :], rz[:], ALU.mult)
+            group_sum(bn_bank[:, 1, half, :], slots(tpn))
+            if half == HALVES - 1:
+                both = [P, HALVES, P]
+                root = keep.tile(both, F32, name="root")
+                nc.scalar.activation(root[:], z_bank[:, 0:HALVES, :], ACT.Abs_reciprocal_sqrt)
+                guess = keep.tile(both, F32, name="guess")
+                nc.scalar.activation(guess[:], root[:], ACT.Square)
+                check = keep.tile(both, F32, name="check")
+                nc.vector.tensor_tensor(check[:], z_bank[:, 0:HALVES, :], guess[:], ALU.mult)
+                neg_rz = keep.tile(both, F32, name="neg_rz")
+                nc.vector.scalar_tensor_tensor(neg_rz[:], check[:], 2.0, guess[:], ALU.subtract, ALU.mult)
+                neg_mean = keep.tile(both, F32, name="neg_mean")
+                nc.vector.tensor_tensor(neg_mean[:], bn_bank[:, 0], neg_rz[:], ALU.mult)
+                shift = keep.tile(both, F32, name="shift")
+                nc.vector.tensor_tensor(shift[:], bn_bank[:, 1], neg_mean[:], ALU.mult)
+                for other in range(HALVES):
+                    nc.tensor.transpose(
+                        back_bank[:, 0, PAIR * other:PAIR * (other + 1), :].rearrange("p t g -> p (t g)"),
+                        neg_rz[:, other, :], identity[:])
+                for t in range(PACK):
+                    nc.scalar.activation(weight[:, t, :], back_bank[:, 0, t, :], ACT.Copy, scale=rs_sb[:, t:t + 1])
+            rows = []
             for part in range(2):
-                rows = slice(part * VOTE // 2, (part + 1) * VOTE // 2)
-                nc.vector.tensor_tensor(tph[:, rows], tpn[:, rows], h[:, rows], ALU.mult)
-            group_sum(acc_bank[:, half, :], [thp, tph])
-            shift = work.tile([P, P], F32, name="shift")
-            nc.vector.tensor_tensor(shift[:], bn_bank[:, half, 1, :], mean[:], ALU.mult)
-            numer = work.tile([P, P], F32, name="numer")
-            nc.vector.tensor_tensor(numer[:], shift[:], acc_bank[:, half, :], ALU.subtract)
-            for t2 in range(PAIR):
-                t = PAIR * half + t2
-                nc.scalar.activation(weight[:, t, :], back_bank[:, 0, t, :], ACT.Copy, scale=rs_sb[:, t:t + 1])
+                first, last = part * VOTE // 2, (part + 1) * VOTE // 2
+                nc.vector.scalar_tensor_tensor(
+                    thp[:, first:last].rearrange("p i t g -> p (i t g)"),
+                    h2[:, first:last].rearrange("p i t g -> p (i t g)"), 1.0,
+                    q[:, first:last].rearrange("p i t g -> p (i t g)"), ALU.subtract, ALU.mult)
+                nc.vector.tensor_tensor(tph[:, first:last], tpn[:, first:last], h[:, first:last], ALU.mult)
+                rows = rows + slots(thp, first, last) + slots(tph, first, last)
+            group_sum(acc[half], rows)
+
+        numer = keep.tile([P, HALVES, P], F32, name="numer")
+        for half in range(HALVES):
+            nc.vector.tensor_tensor(numer[:, half, :], shift[:, half, :], acc[half], ALU.add)
             nc.tensor.transpose(back_bank[:, 1, PAIR * half:PAIR * (half + 1), :].rearrange("p t g -> p (t g)"),
-                                numer[:], identity[:])
+                                numer[:, half, :], identity[:])
 
         wor_grouped = keep.tile([P, PACK * F], BF16, name="wor_grouped", align_bytes=64)
-        dst, src = dealt_views(wor_raw, wor_grouped, 0, P)
-        nc.scalar.copy(dst, src)
+        for piece in range(4):
+            dst, src = dealt_views(wor_raw, wor_grouped, piece * P // 4, (piece + 1) * P // 4)
+            nc.scalar.copy(dst, src)
         wor_codes = keep.tile([P, F], U32, name="wor_codes", align_bytes=64)
         wor_scales = keep.tile([P, F], U8, name="wor_scales", align_bytes=64)
         nc.vector.quantize_mx(wor_codes[:].bitcast(FP8X4), wor_scales[:], wor_grouped[:])

@@ -19,8 +19,6 @@ K, R, F, T, J, G = 512, 512, 512, 2048, 512, 64
 VOTE = J // G
 HALVES = 2
 PAIR = PACK // HALVES
-SPREAD = 8
-W1_SCALAR_SHARE = 64
 
 FLOPS = 2 * K * R * J * 2 + 2 * R * F * G
 
@@ -39,66 +37,65 @@ def tile_attend_tgroupvote_o_pl_kernel(tc, dtab_words, dtab_scales, tab_words, t
         work = ctx.enter_context(tc.tile_pool(name="work", bufs=HALVES))
         psum = ctx.enter_context(tc.psum_pool(name="psum", bufs=1))
 
+        tab_s = keep.tile([P, T], U8, name="tab_s", tag="tab_s_then_res")
+        dtab_s = keep.tile([P, T], U8, name="dtab_s", tag="dtab_s_then_rs")
+        nc.vector.memset(tab_s[:].bitcast(I32), 0)
+        nc.vector.memset(dtab_s[:].bitcast(I32), 0)
+
+        def load_scale_rows(window, scales):
+            for row in range(4):
+                nc.sync.dma_start(window[row:P:32, :].bitcast(I32), scales[0, row:16:4, :].bitcast(I32))
+
         w1_raw = keep.tile([P, PACK, R], F32, name="w1_raw", tag="weights_raw")
         nc.sync.dma_start(w1_raw[:], w1.rearrange("(p t) r -> p t r", t=PACK))
         offsets = keep.tile([P, J // 16], U16, name="offsets")
         nc.sync.dma_start(offsets[:], offs)
-        tab_w = keep.tile([P, T], I32, name="tab_w", tag="tab_w_then_res")
-        nc.sync.dma_start(tab_w[:], tab_words[0].rearrange("p n t -> p (n t)").bitcast(I32))
-        dtab_w = keep.tile([P, T], I32, name="dtab_w", tag="dtab_w_then_rs")
-        nc.sync.dma_start(dtab_w[:], dtab_words[0].rearrange("p n t -> p (n t)").bitcast(I32))
         steep_sb = keep.tile([P, PACK], F32, name="steep_sb")
-        nc.scalar.dma_start(steep_sb[:], steep.rearrange("(p t) o -> p (t o)", t=PACK))
-
-        tab_s = keep.tile([P, T], U8, name="tab_s")
-        dtab_s = keep.tile([P, T], U8, name="dtab_s")
-        nc.vector.memset(tab_s[:].bitcast(I32), 0)
-        planes = keep.tile([P, 2, J], U8, name="planes", align_bytes=64)
-        nc.vector.memset(planes[:].rearrange("p s j -> p (s j)").bitcast(I32), 0)
-        nc.vector.memset(dtab_s[:].bitcast(I32), 0)
-        nc.scalar.dma_start(tab_s[0:P:SPREAD, :].bitcast(I32), tab_scales[0].bitcast(I32))
-        nc.scalar.dma_start(dtab_s[0:P:SPREAD, :].bitcast(I32), dtab_scales[0].bitcast(I32))
+        nc.sync.dma_start(steep_sb[:], steep.rearrange("(p t) o -> p (t o)", t=PACK))
+        load_scale_rows(tab_s, tab_scales)
+        tab_w = keep.tile([P, T], I32, name="tab_w", tag="tab_w_then_dtab_gs", align_bytes=64)
+        nc.sync.dma_start(tab_w[:], tab_words[0].rearrange("p n t -> p (n t)").bitcast(I32))
+        load_scale_rows(dtab_s, dtab_scales)
+        dtab_w = keep.tile([P, T], I32, name="dtab_w", tag="dtab_w_then_ph")
+        nc.sync.dma_start(dtab_w[:], dtab_words[0].rearrange("p n t -> p (n t)").bitcast(I32))
 
         identity = keep.tile([P, P], F32, name="identity")
         make_identity(nc, identity[:])
         neg_steep = keep.tile([P, PACK], F32, name="neg_steep")
-        nc.vector.tensor_scalar(neg_steep[:], steep_sb[:], -1.0, None, ALU.mult)
+        nc.gpsimd.tensor_scalar(neg_steep[:], steep_sb[:], -1.0, 0.0, ALU.mult, ALU.add)
 
         w1_grouped = keep.tile([P, PACK * R], BF16, name="w1_grouped", align_bytes=64)
-        dst, src = dealt_views(w1_raw, w1_grouped, 0, W1_SCALAR_SHARE)
-        nc.scalar.copy(dst, src)
-
-        listed_s = keep.tile([P, 2, J], U8, name="listed_s")
-        nc.vector.tensor_copy(listed_s[:, 0, :], tab_s[:].indirect(offsets[:]))
-        nc.vector.tensor_copy(listed_s[:, 1, :], dtab_s[:].indirect(offsets[:]))
-        for row in range(4):
-            nc.scalar.dma_start(planes[row:P:32].rearrange("p s j -> p (s j)").bitcast(I32),
-                                listed_s[SPREAD * row:P:32].rearrange("p s j -> p (s j)").bitcast(I32))
-
-        dst, src = dealt_views(w1_raw, w1_grouped, W1_SCALAR_SHARE, P)
+        dst, src = dealt_views(w1_raw, w1_grouped, 0, P)
         nc.vector.tensor_copy(dst, src)
+        tab_gs = keep.tile([P, J], U8, name="tab_gs", align_bytes=64)
+        nc.vector.tensor_copy(tab_gs[:], tab_s[:].indirect(offsets[:]))
         w1_codes = keep.tile([P, R], U32, name="w1_codes", align_bytes=64)
         w1_scales = keep.tile([P, R], U8, name="w1_scales", align_bytes=64)
         nc.vector.quantize_mx(w1_codes[:].bitcast(FP8X4), w1_scales[:], w1_grouped[:])
 
         tab_gw = keep.tile([P, J], U32, name="tab_gw", align_bytes=64)
         nc.vector.tensor_copy(tab_gw[:], tab_w[:].bitcast(U32).indirect(offsets[:]))
+        dtab_gs = keep.tile([P, J], U8, name="dtab_gs", tag="tab_w_then_dtab_gs", align_bytes=64)
+        nc.vector.tensor_copy(dtab_gs[:], dtab_s[:].indirect(offsets[:]))
         dtab_gw = keep.tile([P, J], U32, name="dtab_gw", align_bytes=64)
         nc.vector.tensor_copy(dtab_gw[:], dtab_w[:].bitcast(U32).indirect(offsets[:]))
 
         wor_raw = keep.tile([P, PACK, F], F32, name="wor_raw", tag="weights_raw")
         nc.sync.dma_start(wor_raw[:], wor.rearrange("(p t) f -> p t f", t=PACK))
-        res_sb = keep.tile([P, PACK, G], F32, name="res_sb", tag="tab_w_then_res")
+        res_sb = keep.tile([P, PACK, G], F32, name="res_sb", tag="tab_s_then_res")
         nc.sync.dma_start(res_sb[:], res.rearrange("(p j) g -> p j g", j=PACK))
-        rs_sb = keep.tile([P, PACK], F32, name="rs_sb", tag="dtab_w_then_rs")
+        rs_sb = keep.tile([P, PACK], F32, name="rs_sb", tag="dtab_s_then_rs")
         nc.sync.dma_start(rs_sb[:], rs.rearrange("(p t) o -> p (t o)", t=PACK))
 
         z_bank = psum.tile([P, HALVES + 1, P], F32, name="z_bank")
-        bn_bank = psum.tile([P, 2, HALVES, P], F32, name="bn_bank")
+        a_banks = [psum.tile([P, J], F32, name="a_bank%d" % n) for n in range(PAIR)]
+        ta_banks = [psum.tile([P, J], F32, name="ta_bank%d" % n) for n in range(PAIR + 1)]
+        bn_bank = ta_banks[0][:].rearrange("p (s h m) -> p s h m", s=2, h=HALVES)
+        ta_of = [0, 1, 2, 1]
         acc_bank = psum.tile([P, P], F32, name="acc_bank")
         acc = [z_bank[:, HALVES, :], acc_bank[:]]
-        back_bank = psum.tile([P, 2, PACK, G], F32, name="back_bank")
-        weight = keep.tile([P, PACK, G], F32, name="weight")
+        back_bank = psum.tile([P, PACK, G], F32, name="back_bank")
+        weight = keep.tile([P, G, PACK], F32, name="weight")
 
         def group_sum(out, rows):
             for n, row in enumerate(rows):
@@ -108,8 +105,7 @@ def tile_attend_tgroupvote_o_pl_kernel(tc, dtab_words, dtab_scales, tab_words, t
         def slots(tile, first=0, last=VOTE):
             return [tile[:, i] for i in range(first, last)]
 
-        def first_layer(name, t, words, plane):
-            bank = psum.tile([P, J], F32, name=name, bufs=2)
+        def first_layer(bank, t, words, plane):
             cols = slice(t * P, (t + 1) * P)
             nc.tensor.matmul_mx(bank[:], w1_codes[:, cols].bitcast(FP8X4), w1_scales[:, cols],
                                 words[:].bitcast(FP8X4), plane, start=True, stop=True)
@@ -120,18 +116,18 @@ def tile_attend_tgroupvote_o_pl_kernel(tc, dtab_words, dtab_scales, tab_words, t
 
         for half in range(HALVES):
             shape = [P, VOTE, PAIR, G]
-            p = work.tile(shape, F32, name="p")
+            p = keep.tile(shape, F32, name="p")
             h = work.tile(shape, F32, name="h")
             slope = work.tile(shape, F32, name="slope")
             h2 = work.tile(shape, F32, name="h2")
             q = work.tile(shape, F32, name="q")
-            ph = work.tile(shape, F32, name="ph")
+            ph = keep.tile(shape, F32, name="ph", tag="dtab_w_then_ph")
             tpn = work.tile(shape, F32, name="tpn")
             thp = work.tile(shape, F32, name="thp")
             tph = work.tile(shape, F32, name="tph")
             for t2 in range(PAIR):
                 t = PAIR * half + t2
-                a = first_layer("a_bank", t, tab_gw, planes[:, 0, :])
+                a = first_layer(a_banks[t2], t, tab_gw, tab_gs[:])
                 nc.scalar.activation(p[:, :, t2, :], a, ACT.Sigmoid, scale=steep_sb[:, t:t + 1])
                 nc.scalar.activation(h[:, :, t2, :], a, ACT.Tanh)
             for t2 in range(PAIR):
@@ -142,32 +138,29 @@ def tile_attend_tgroupvote_o_pl_kernel(tc, dtab_words, dtab_scales, tab_words, t
             group_sum(z_bank[:, half, :], slots(p))
             for t2 in range(PAIR):
                 t = PAIR * half + t2
-                ta = first_layer("ta_bank", t, dtab_gw, planes[:, 1, :])
+                ta = first_layer(ta_banks[ta_of[t]], t, dtab_gw, dtab_gs[:])
                 nc.vector.tensor_tensor(q[:, :, t2, :], ta, p[:, :, t2, :], ALU.mult)
-            nc.vector.tensor_tensor(flat(ph), flat(p), flat(h), ALU.mult)
+            for t2 in range(PAIR):
+                nc.vector.tensor_tensor(ph[:, :, t2, :], p[:, :, t2, :], h[:, :, t2, :], ALU.mult)
             group_sum(bn_bank[:, 0, half, :], slots(ph))
             nc.vector.tensor_tensor(flat(tpn), flat(slope), flat(q), ALU.mult)
             group_sum(bn_bank[:, 1, half, :], slots(tpn))
             if half == HALVES - 1:
                 both = [P, HALVES, P]
-                root = keep.tile(both, F32, name="root")
+                root = keep.tile(both, F32, name="root", tag="root_then_wor", align_bytes=64)
                 nc.scalar.activation(root[:], z_bank[:, 0:HALVES, :], ACT.Abs_reciprocal_sqrt)
-                guess = keep.tile(both, F32, name="guess")
-                nc.scalar.activation(guess[:], root[:], ACT.Square)
-                check = keep.tile(both, F32, name="check")
-                nc.vector.tensor_tensor(check[:], z_bank[:, 0:HALVES, :], guess[:], ALU.mult)
-                neg_rz = keep.tile(both, F32, name="neg_rz")
-                nc.vector.scalar_tensor_tensor(neg_rz[:], check[:], 2.0, guess[:], ALU.subtract, ALU.mult)
-                neg_mean = keep.tile(both, F32, name="neg_mean")
-                nc.vector.tensor_tensor(neg_mean[:], bn_bank[:, 0], neg_rz[:], ALU.mult)
+                rz = keep.tile(both, F32, name="rz")
+                nc.scalar.activation(rz[:], root[:], ACT.Square)
+                mean = keep.tile(both, F32, name="mean")
+                nc.vector.tensor_tensor(mean[:], bn_bank[:, 0], rz[:], ALU.mult)
                 shift = keep.tile(both, F32, name="shift")
-                nc.vector.tensor_tensor(shift[:], bn_bank[:, 1], neg_mean[:], ALU.mult)
+                nc.vector.tensor_tensor(shift[:], bn_bank[:, 1], mean[:], ALU.mult)
+                rz_back = ta_banks[2][:, 0:PACK * G].rearrange("p (t g) -> p t g", t=PACK)
                 for other in range(HALVES):
-                    nc.tensor.transpose(
-                        back_bank[:, 0, PAIR * other:PAIR * (other + 1), :].rearrange("p t g -> p (t g)"),
-                        neg_rz[:, other, :], identity[:])
-                for t in range(PACK):
-                    nc.scalar.activation(weight[:, t, :], back_bank[:, 0, t, :], ACT.Copy, scale=rs_sb[:, t:t + 1])
+                    nc.tensor.transpose(rz_back[:, PAIR * other:PAIR * (other + 1), :].rearrange("p t g -> p (t g)"),
+                                        rz[:, other, :], identity[:])
+                nc.vector.tensor_tensor(weight[:], rz_back.rearrange("p t g -> p g t"),
+                                        rs_sb[:].unsqueeze(1).to_broadcast([P, G, PACK]), ALU.mult)
             rows = []
             for part in range(2):
                 first, last = part * VOTE // 2, (part + 1) * VOTE // 2
@@ -181,36 +174,36 @@ def tile_attend_tgroupvote_o_pl_kernel(tc, dtab_words, dtab_scales, tab_words, t
 
         numer = keep.tile([P, HALVES, P], F32, name="numer")
         for half in range(HALVES):
-            nc.vector.tensor_tensor(numer[:, half, :], shift[:, half, :], acc[half], ALU.add)
-            nc.tensor.transpose(back_bank[:, 1, PAIR * half:PAIR * (half + 1), :].rearrange("p t g -> p (t g)"),
+            nc.vector.tensor_tensor(numer[:, half, :], shift[:, half, :], acc[half], ALU.subtract)
+            nc.tensor.transpose(back_bank[:, PAIR * half:PAIR * (half + 1), :].rearrange("p t g -> p (t g)"),
                                 numer[:, half, :], identity[:])
 
-        wor_grouped = keep.tile([P, PACK * F], BF16, name="wor_grouped", align_bytes=64)
-        for piece in range(4):
-            dst, src = dealt_views(wor_raw, wor_grouped, piece * P // 4, (piece + 1) * P // 4)
-            nc.scalar.copy(dst, src)
+        wor_grouped = keep.tile([P, PACK * F], BF16, name="wor_grouped", tag="root_then_wor", align_bytes=64)
+        dst, src = dealt_views(wor_raw, wor_grouped, 0, P)
+        nc.scalar.copy(dst, src)
         wor_codes = keep.tile([P, F], U32, name="wor_codes", align_bytes=64)
         wor_scales = keep.tile([P, F], U8, name="wor_scales", align_bytes=64)
         nc.vector.quantize_mx(wor_codes[:].bitcast(FP8X4), wor_scales[:], wor_grouped[:])
 
+        res_grouped = keep.tile([P, G, PACK], F32, name="res_grouped")
+        nc.scalar.copy(res_grouped[:], res_sb[:].rearrange("p j g -> p g j"))
+
         fo_grouped = keep.tile([P, G, PACK], BF16, name="fo_grouped", align_bytes=64)
-        nc.vector.tensor_tensor(fo_grouped[:], back_bank[:, 1].rearrange("p t g -> p g t"),
-                                weight[:].rearrange("p t g -> p g t"), ALU.mult)
+        nc.vector.tensor_tensor(fo_grouped[:], back_bank[:].rearrange("p t g -> p g t"), weight[:], ALU.mult)
         fo_codes = keep.tile([P, G], U32, name="fo_codes", align_bytes=64)
         fo_scales = keep.tile([P, G], U8, name="fo_scales", align_bytes=64)
         nc.vector.quantize_mx(fo_codes[:].bitcast(FP8X4), fo_scales[:], fo_grouped[:].rearrange("p g t -> p (g t)"))
 
-        yo = psum.tile([P, PACK, G], F32, name="a_bank", bufs=2)
+        yo = a_banks[0][:, 0:PACK * G].rearrange("p (j g) -> p j g", j=PACK)
         for j in range(PACK):
             cols = slice(j * P, (j + 1) * P)
             nc.tensor.matmul_mx(yo[:, j, :], wor_codes[:, cols].bitcast(FP8X4), wor_scales[:, cols],
                                 fo_codes[:].bitcast(FP8X4), fo_scales[:], start=True, stop=True)
 
         y_grouped = keep.tile([P, G, PACK], BF16, name="y_grouped", align_bytes=64)
-        nc.vector.tensor_tensor(y_grouped[:], yo[:].rearrange("p j g -> p g j"),
-                                res_sb[:].rearrange("p j g -> p g j"), ALU.add)
+        nc.vector.tensor_tensor(y_grouped[:], yo.rearrange("p j g -> p g j"), res_grouped[:], ALU.add)
         y = keep.tile([P, PACK, G], F32, name="y")
-        nc.vector.tensor_tensor(y[:], yo[:], res_sb[:], ALU.add)
+        nc.vector.tensor_tensor(y[:], yo, res_sb[:], ALU.add)
         nc.sync.dma_start(out_0.rearrange("(p j) g -> p j g", j=PACK), y[:])
         y_codes = keep.tile([P, G], I32, name="y_codes", align_bytes=64)
         y_scales = keep.tile([P, G], U8, name="y_scales", align_bytes=64)

from contextlib import ExitStack

import concourse.mybir as mybir
from concourse.masks import make_identity

F32 = mybir.dt.float32
BF16 = mybir.dt.bfloat16
I32 = mybir.dt.int32
U32 = mybir.dt.uint32
U16 = mybir.dt.uint16
U8 = mybir.dt.uint8
FP8X4 = mybir.dt.float8_e4m3fn_x4
ALU = mybir.AluOpType
ACT = mybir.ActivationFunctionType

P = 128
PACK = 4
K, R, F, T, J, G = 512, 512, 512, 2048, 512, 64
VOTE = J // G
HALVES = 2
PAIR = PACK // HALVES

FLOPS = 2 * K * R * J * 2 + 2 * R * F * G


def dealt_views(raw, grouped, m0, m1):
    src = raw[:].rearrange("p t (m j) -> p m t j", j=PACK)[:, m0:m1]
    dst = grouped[:].rearrange("p (j m t) -> p m t j", j=PACK, t=PACK)[:, m0:m1]
    return dst, src


def tile_attend_tgroupvote_o_pl_kernel(tc, dtab_words, dtab_scales, tab_words, tab_scales, w1, steep, rs, wor, res, offs,
                                        out_0, out_1, out_2):
    nc = tc.nc
    with ExitStack() as ctx:
        keep = ctx.enter_context(tc.tile_pool(name="keep", bufs=1))
        work = ctx.enter_context(tc.tile_pool(name="work", bufs=HALVES))
        psum = ctx.enter_context(tc.psum_pool(name="psum", bufs=1))

        tab_s = keep.tile([P, T], U8, name="tab_s", tag="tab_s_then_res")
        dtab_s = keep.tile([P, T], U8, name="dtab_s", tag="dtab_s_then_rs")
        nc.vector.memset(tab_s[:].bitcast(I32), 0)
        nc.vector.memset(dtab_s[:].bitcast(I32), 0)

        def load_scale_rows(window, scales):
            for row in range(4):
                nc.sync.dma_start(window[row:P:32, :].bitcast(I32), scales[0, row:16:4, :].bitcast(I32))

        w1_raw = keep.tile([P, PACK, R], F32, name="w1_raw", tag="weights_raw")
        nc.sync.dma_start(w1_raw[:], w1.rearrange("(p t) r -> p t r", t=PACK))
        offsets = keep.tile([P, J // 16], U16, name="offsets")
        nc.sync.dma_start(offsets[:], offs)
        steep_sb = keep.tile([P, PACK], F32, name="steep_sb")
        nc.sync.dma_start(steep_sb[:], steep.rearrange("(p t) o -> p (t o)", t=PACK))
        load_scale_rows(tab_s, tab_scales)
        tab_w = keep.tile([P, T], I32, name="tab_w", tag="tab_w_then_dtab_gs", align_bytes=64)
        nc.sync.dma_start(tab_w[:], tab_words[0].rearrange("p n t -> p (n t)").bitcast(I32))
        load_scale_rows(dtab_s, dtab_scales)
        dtab_w = keep.tile([P, T], I32, name="dtab_w", tag="dtab_w_then_ph")
        nc.sync.dma_start(dtab_w[:], dtab_words[0].rearrange("p n t -> p (n t)").bitcast(I32))

        identity = keep.tile([P, P], F32, name="identity")
        make_identity(nc, identity[:])
        neg_steep = keep.tile([P, PACK], F32, name="neg_steep")
        nc.gpsimd.tensor_scalar(neg_steep[:], steep_sb[:], -1.0, 0.0, ALU.mult, ALU.add)

        w1_grouped = keep.tile([P, PACK * R], BF16, name="w1_grouped", align_bytes=64)
        dst, src = dealt_views(w1_raw, w1_grouped, 0, P)
        nc.vector.tensor_copy(dst, src)
        tab_gs = keep.tile([P, J], U8, name="tab_gs", align_bytes=64)
        nc.vector.tensor_copy(tab_gs[:], tab_s[:].indirect(offsets[:]))
        w1_codes = keep.tile([P, R], U32, name="w1_codes", align_bytes=64)
        w1_scales = keep.tile([P, R], U8, name="w1_scales", align_bytes=64)
        nc.vector.quantize_mx(w1_codes[:].bitcast(FP8X4), w1_scales[:], w1_grouped[:])

        tab_gw = keep.tile([P, J], U32, name="tab_gw", align_bytes=64)
        nc.vector.tensor_copy(tab_gw[:], tab_w[:].bitcast(U32).indirect(offsets[:]))
        dtab_gs = keep.tile([P, J], U8, name="dtab_gs", tag="tab_w_then_dtab_gs", align_bytes=64)
        nc.vector.tensor_copy(dtab_gs[:], dtab_s[:].indirect(offsets[:]))
        dtab_gw = keep.tile([P, J], U32, name="dtab_gw", align_bytes=64)
        nc.vector.tensor_copy(dtab_gw[:], dtab_w[:].bitcast(U32).indirect(offsets[:]))

        wor_raw = keep.tile([P, PACK, F], F32, name="wor_raw", tag="weights_raw")
        nc.sync.dma_start(wor_raw[:], wor.rearrange("(p t) f -> p t f", t=PACK))
        res_sb = keep.tile([P, PACK, G], F32, name="res_sb", tag="tab_s_then_res")
        nc.sync.dma_start(res_sb[:], res.rearrange("(p j) g -> p j g", j=PACK))
        rs_sb = keep.tile([P, PACK], F32, name="rs_sb", tag="dtab_s_then_rs")
        nc.sync.dma_start(rs_sb[:], rs.rearrange("(p t) o -> p (t o)", t=PACK))

        z_bank = psum.tile([P, HALVES + 1, P], F32, name="z_bank")
        a_banks = [psum.tile([P, J], F32, name="a_bank%d" % n) for n in range(PAIR)]
        ta_banks = [psum.tile([P, J], F32, name="ta_bank%d" % n) for n in range(PAIR + 1)]
        bn_bank = ta_banks[0][:].rearrange("p (s h m) -> p s h m", s=2, h=HALVES)
        ta_of = [0, 1, 2, 1]
        acc_bank = psum.tile([P, P], F32, name="acc_bank")
        acc = [z_bank[:, HALVES, :], acc_bank[:]]
        back_bank = psum.tile([P, PACK, G], F32, name="back_bank")
        weight = keep.tile([P, G, PACK], F32, name="weight")

        def group_sum(out, rows):
            for n, row in enumerate(rows):
                nc.tensor.matmul(out, row.rearrange("p t g -> p (t g)"), identity[:], is_transpose=True,
                                 start=(n == 0), stop=(n == len(rows) - 1))

        def slots(tile, first=0, last=VOTE):
            return [tile[:, i] for i in range(first, last)]

        def first_layer(bank, t, words, plane):
            cols = slice(t * P, (t + 1) * P)
            nc.tensor.matmul_mx(bank[:], w1_codes[:, cols].bitcast(FP8X4), w1_scales[:, cols],
                                words[:].bitcast(FP8X4), plane, start=True, stop=True)
            return bank[:].rearrange("p (g i) -> p i g", i=VOTE)

        def flat(tile):
            return tile[:].rearrange("p i t g -> p (i t g)")

        for half in range(HALVES):
            shape = [P, VOTE, PAIR, G]
            p = keep.tile(shape, F32, name="p")
            h = work.tile(shape, F32, name="h")
            slope = work.tile(shape, F32, name="slope")
            h2 = work.tile(shape, F32, name="h2")
            q = work.tile(shape, F32, name="q")
            ph = keep.tile(shape, F32, name="ph", tag="dtab_w_then_ph")
            tpn = work.tile(shape, F32, name="tpn")
            thp = work.tile(shape, F32, name="thp")
            tph = work.tile(shape, F32, name="tph")
            for t2 in range(PAIR):
                t = PAIR * half + t2
                a = first_layer(a_banks[t2], t, tab_gw, tab_gs[:])
                nc.scalar.activation(p[:, :, t2, :], a, ACT.Sigmoid, scale=steep_sb[:, t:t + 1])
                nc.scalar.activation(h[:, :, t2, :], a, ACT.Tanh)
            for t2 in range(PAIR):
                t = PAIR * half + t2
                nc.scalar.activation(slope[:, :, t2, :], p[:, :, t2, :], ACT.Identity,
                                     scale=steep_sb[:, t:t + 1], bias=neg_steep[:, t:t + 1])
            nc.scalar.activation(flat(h2), flat(h), ACT.Square)
            group_sum(z_bank[:, half, :], slots(p))
            for t2 in range(PAIR):
                t = PAIR * half + t2
                ta = first_layer(ta_banks[ta_of[t]], t, dtab_gw, dtab_gs[:])
                nc.vector.tensor_tensor(q[:, :, t2, :], ta, p[:, :, t2, :], ALU.mult)
            for t2 in range(PAIR):
                nc.vector.tensor_tensor(ph[:, :, t2, :], p[:, :, t2, :], h[:, :, t2, :], ALU.mult)
            group_sum(bn_bank[:, 0, half, :], slots(ph))
            nc.vector.tensor_tensor(flat(tpn), flat(slope), flat(q), ALU.mult)
            group_sum(bn_bank[:, 1, half, :], slots(tpn))
            if half == HALVES - 1:
                both = [P, HALVES, P]
                root = keep.tile(both, F32, name="root", tag="root_then_wor", align_bytes=64)
                nc.scalar.activation(root[:], z_bank[:, 0:HALVES, :], ACT.Abs_reciprocal_sqrt)
                rz = keep.tile(both, F32, name="rz")
                nc.scalar.activation(rz[:], root[:], ACT.Square)
                mean = keep.tile(both, F32, name="mean")
                nc.vector.tensor_tensor(mean[:], bn_bank[:, 0], rz[:], ALU.mult)
                shift = keep.tile(both, F32, name="shift")
                nc.vector.tensor_tensor(shift[:], bn_bank[:, 1], mean[:], ALU.mult)
                rz_back = ta_banks[2][:, 0:PACK * G].rearrange("p (t g) -> p t g", t=PACK)
                for other in range(HALVES):
                    nc.tensor.transpose(rz_back[:, PAIR * other:PAIR * (other + 1), :].rearrange("p t g -> p (t g)"),
                                        rz[:, other, :], identity[:])
                nc.vector.tensor_tensor(weight[:], rz_back.rearrange("p t g -> p g t"),
                                        rs_sb[:].unsqueeze(1).to_broadcast([P, G, PACK]), ALU.mult)
            rows = []
            for part in range(2):
                first, last = part * VOTE // 2, (part + 1) * VOTE // 2
                nc.vector.scalar_tensor_tensor(
                    thp[:, first:last].rearrange("p i t g -> p (i t g)"),
                    h2[:, first:last].rearrange("p i t g -> p (i t g)"), 1.0,
                    q[:, first:last].rearrange("p i t g -> p (i t g)"), ALU.subtract, ALU.mult)
                nc.vector.tensor_tensor(tph[:, first:last], tpn[:, first:last], h[:, first:last], ALU.mult)
                rows = rows + slots(thp, first, last) + slots(tph, first, last)
            group_sum(acc[half], rows)

        numer = keep.tile([P, HALVES, P], F32, name="numer")
        for half in range(HALVES):
            nc.vector.tensor_tensor(numer[:, half, :], shift[:, half, :], acc[half], ALU.subtract)
            nc.tensor.transpose(back_bank[:, PAIR * half:PAIR * (half + 1), :].rearrange("p t g -> p (t g)"),
                                numer[:, half, :], identity[:])

        wor_grouped = keep.tile([P, PACK * F], BF16, name="wor_grouped", tag="root_then_wor", align_bytes=64)
        dst, src = dealt_views(wor_raw, wor_grouped, 0, P)
        nc.scalar.copy(dst, src)
        wor_codes = keep.tile([P, F], U32, name="wor_codes", align_bytes=64)
        wor_scales = keep.tile([P, F], U8, name="wor_scales", align_bytes=64)
        nc.vector.quantize_mx(wor_codes[:].bitcast(FP8X4), wor_scales[:], wor_grouped[:])

        res_grouped = keep.tile([P, G, PACK], F32, name="res_grouped")
        nc.scalar.copy(res_grouped[:], res_sb[:].rearrange("p j g -> p g j"))

        fo_grouped = keep.tile([P, G, PACK], BF16, name="fo_grouped", align_bytes=64)
        nc.vector.tensor_tensor(fo_grouped[:], back_bank[:].rearrange("p t g -> p g t"), weight[:], ALU.mult)
        fo_codes = keep.tile([P, G], U32, name="fo_codes", align_bytes=64)
        fo_scales = keep.tile([P, G], U8, name="fo_scales", align_bytes=64)
        nc.vector.quantize_mx(fo_codes[:].bitcast(FP8X4), fo_scales[:], fo_grouped[:].rearrange("p g t -> p (g t)"))

        yo = a_banks[0][:, 0:PACK * G].rearrange("p (j g) -> p j g", j=PACK)
        for j in range(PACK):
            cols = slice(j * P, (j + 1) * P)
            nc.tensor.matmul_mx(yo[:, j, :], wor_codes[:, cols].bitcast(FP8X4), wor_scales[:, cols],
                                fo_codes[:].bitcast(FP8X4), fo_scales[:], start=True, stop=True)

        y_grouped = keep.tile([P, G, PACK], BF16, name="y_grouped", align_bytes=64)
        nc.vector.tensor_tensor(y_grouped[:], yo.rearrange("p j g -> p g j"), res_grouped[:], ALU.add)
        y = keep.tile([P, PACK, G], F32, name="y")
        nc.vector.tensor_tensor(y[:], yo, res_sb[:], ALU.add)
        nc.sync.dma_start(out_0.rearrange("(p j) g -> p j g", j=PACK), y[:])
        y_codes = keep.tile([P, G], I32, name="y_codes", align_bytes=64)
        y_scales = keep.tile([P, G], U8, name="y_scales", align_bytes=64)
        nc.vector.quantize_mx(y_codes[:].bitcast(FP8X4), y_scales[:], y_grouped[:].rearrange("p g j -> p (g j)"))
        nc.scalar.dma_start(out_1[0].rearrange("p c t -> p (c t)").bitcast(I32), y_codes[:])
        for quad in range(4):
            queue = nc.sync if quad % 2 == 0 else nc.scalar
            queue.dma_start(out_2[0, 4 * quad:4 * quad + 4, :].bitcast(I32),
                            y_scales[32 * quad:32 * quad + 4, :].bitcast(I32))
